import numpy as np
import ml_dtypes


def mxq(x, axis, fmt="e4m3"):
    dtype, down = {"e4m3": (ml_dtypes.float8_e4m3fn, 7), "e5m2": (ml_dtypes.float8_e5m2, 14)}[fmt]
    v = np.moveaxis(np.asarray(x, np.float32).astype(ml_dtypes.bfloat16).astype(np.float64), axis, -1)
    blocks = v.reshape(v.shape[:-1] + (-1, 32))
    amax = np.abs(blocks).max(-1, keepdims=True)
    byte = np.maximum(np.where(amax > 0, np.frexp(amax)[1] - 1 + 127, 0) - down, 1)
    scale = np.exp2(byte - 127.0)
    codes = (blocks / scale).astype(np.float32).astype(dtype).astype(np.float64)
    return np.moveaxis((codes * scale).reshape(v.shape), -1, axis)


WIDE = False


def mx_kscale(k):
    if not WIDE:
        return np.ones(k)
    levels = np.array([10, -10, 5, -5, 0])
    if k % 512:
        return np.exp2(np.random.permutation(np.resize(levels, k // 32))).repeat(32)
    a = np.empty((k // 512, 16))
    for p in range(k // 512):
        a[p, :8] = np.random.permutation(np.resize(levels, 8))
        for g in range(8):
            far = levels[np.abs(levels - a[p, g]) >= 10]
            a[p, g + 8] = far[np.random.randint(len(far))]
    return np.exp2(a.ravel()).repeat(32)


def f64(x):
    return np.asarray(x).astype(np.float64)


def striped(idx):
    return np.tile(np.asarray(idx).reshape(-1, 16).T, (8, 1)).astype(np.uint16)


def unstriped(offs):
    return offs[:16].T.reshape(-1).astype(np.int64)


E2M1 = np.array([0.0, 0.5, 1.0, 1.5, 2.0, 3.0, 4.0, 6.0, -0.0, -0.5, -1.0, -1.5, -2.0, -3.0, -4.0, -6.0])


def pack_weight(w, fmt):
    k, n = w.shape
    w = f64(np.asarray(w, np.float32).astype(ml_dtypes.bfloat16)).reshape(k // 32, 32, n)
    amax = np.abs(w).max(1)
    if fmt == "e4m3":
        byte = np.frexp(amax)[1] - 1 + 127 - 7
    else:
        mant, ex = np.frexp(amax / 6.0)
        byte = np.where(mant > 0.5, ex, ex - 1) + 127
    byte = np.clip(np.where(amax > 0, byte, 1), 1, 254)
    scaled = (w * np.exp2(127.0 - byte)[:, None, :]).reshape(k, n).astype(np.float32)
    by_word = np.ascontiguousarray(scaled.reshape(k // 512, 128, 4, n).transpose(0, 1, 3, 2))
    if fmt == "e4m3":
        words = by_word.astype(ml_dtypes.float8_e4m3fn).view(np.uint8)
    else:
        c = by_word.astype(ml_dtypes.float4_e2m1fn).view(np.uint8) & 0xF
        words = (c[..., 0::2] | (c[..., 1::2] << 4)).reshape(k // 512, 128, 2 * n)
    return np.ascontiguousarray(words), np.ascontiguousarray(byte.astype(np.uint8).reshape(k // 512, 16, n))


def unpack_weight(words, scales, fmt):
    g, _, n = scales.shape
    words = np.ascontiguousarray(words).reshape(g, 128, n, -1)
    if fmt == "e4m3":
        vals = words.view(ml_dtypes.float8_e4m3fn).astype(np.float64)
    else:
        nib = np.empty((g, 128, n, 4), np.uint8)
        nib[..., 0::2] = words & 0xF
        nib[..., 1::2] = words >> 4
        vals = E2M1[nib]
    vals = vals * np.repeat(np.exp2(scales.astype(np.float64) - 127.0), 8, axis=1)[..., None]
    return vals.transpose(0, 1, 3, 2).reshape(g * 512, n)


K, T, J, I, N = 512, 2048, 1024, 512, 512


def setup_inputs():
    n = np.random.standard_normal
    idx = np.random.permutation(T)[:J]
    idx2 = np.random.permutation(J)[:I]
    fk = mx_kscale(K)
    wap = pack_weight(n((K, N)) * 1 / np.sqrt(K) * fk[:, None], "e2m1")
    wbp = pack_weight(n((K, N)) * 1 / np.sqrt(K) * fk[:, None], "e4m3")
    return {
        "xf": (n((K, T)) / fk[:, None]).astype(np.float32),
        "wa_words": wap[0],
        "wa_scales": wap[1],
        "wb_words": wbp[0],
        "wb_scales": wbp[1],
        "offs": striped(idx),
        "offs2": striped(idx2),
    }


def reference(xf, wa_words, wa_scales, wb_words, wb_scales, offs, offs2):
    idx = unstriped(offs)
    idx2 = unstriped(offs2)
    wau = unpack_weight(wa_words, wa_scales, "e2m1")
    wbu = unpack_weight(wb_words, wb_scales, "e4m3")
    xg = f64(xf)[:, idx]
    xgq = mxq(xg, 0, "e4m3")
    p = wau.T @ xgq
    xgidx2q = mxq(xg[:, idx2], 0, "e4m3")
    q = wbu.T @ xgidx2q
    qs = np.zeros((N, J))
    qs[:, idx2] = q
    y = p + qs
    return y

@@ -1,0 +1,145 @@
+from contextlib import ExitStack
+
+import concourse.mybir as mybir
+
+K, T, J, I, N = 512, 2048, 1024, 512, 512
+FLOPS = 2 * K * N * (J + I)
+
+F32 = mybir.dt.float32
+BF16 = mybir.dt.bfloat16
+I32 = mybir.dt.int32
+U32 = mybir.dt.uint32
+U16 = mybir.dt.uint16
+U8 = mybir.dt.uint8
+FP8X4 = mybir.dt.float8_e4m3fn_x4
+FP4X4 = mybir.dt.float4_e2m1fn_x4
+ADD = mybir.AluOpType.add
+
+P = 128
+PACK = 4
+BANK = 512
+HALF = I // 2
+TILES = N // P
+LINE = 4
+
+
+def interleave(nc, dst, planes, width):
+    nc.scalar.copy(
+        out=dst.rearrange("p (c i t) -> p c t i", i=LINE, t=PACK),
+        in_=planes.rearrange("p t (c i) -> p c t i", i=LINE),
+    )
+
+
+def tile_list_two_level_routing_kernel(tc, xf, wa_words, wa_scales, wb_words, wb_scales, offs, offs2, out):
+    nc = tc.nc
+    with ExitStack() as ctx:
+        keep = ctx.enter_context(tc.tile_pool(name="keep", bufs=1))
+        stage = ctx.enter_context(tc.tile_pool(name="stage", bufs=4))
+        q_psum = ctx.enter_context(tc.psum_pool(name="q_psum", bufs=4))
+        p_psum = ctx.enter_context(tc.psum_pool(name="p_psum", bufs=4))
+
+        list1 = keep.tile([P, J // 16], U16, name="list1")
+        list2 = keep.tile([P, I // 16], U16, name="list2")
+        wa_codes = keep.tile([P, 2 * N], U8, name="wa_codes", align_bytes=64)
+        wb_codes = keep.tile([P, N], U32, name="wb_codes", align_bytes=64)
+        wa_sc = keep.tile([P, N], U8, name="wa_sc", align_bytes=64)
+        wb_sc = keep.tile([P, N], U8, name="wb_sc", align_bytes=64)
+        nc.vector.memset(wb_sc[:].bitcast(U32), 0)
+        nc.vector.memset(wa_sc[:].bitcast(U32), 0)
+
+        x_rows = xf.rearrange("(p t) c -> p t c", t=PACK)
+        x_planes = [keep.tile([P, T], F32, name="x%d" % t, tag="x%d" % t, align_bytes=64) for t in range(PACK)]
+        nc.sync.dma_start(out=x_planes[0][:], in_=x_rows[:, 0, :])
+        nc.sync.dma_start(list1[:], offs)
+        for t in range(1, PACK):
+            nc.sync.dma_start(out=x_planes[t][:], in_=x_rows[:, t, :])
+        nc.sync.dma_start(list2[:], offs2)
+        nc.sync.dma_start(out=wb_codes[:].bitcast(I32), in_=wb_words[0].rearrange("p n t -> p (n t)").bitcast(I32))
+        for quad in range(4):
+            nc.sync.dma_start(out=wb_sc[32 * quad : 32 * quad + 4, :].bitcast(I32),
+                              in_=wb_scales[0, 4 * quad : 4 * quad + 4, :].bitcast(I32))
+        nc.sync.dma_start(out=wa_codes[:].bitcast(I32), in_=wa_words[0].bitcast(I32))
+        for quad in range(4):
+            nc.sync.dma_start(out=wa_sc[32 * quad : 32 * quad + 4, :].bitcast(I32),
+                              in_=wa_scales[0, 4 * quad : 4 * quad + 4, :].bitcast(I32))
+
+        pages = [keep.tile([P, J], F32, name="page%d" % m) for m in range(TILES)]
+        for m in range(TILES):
+            nc.gpsimd.memset(pages[m][:], 0.0)
+
+        xg = keep.tile([P, PACK * J], F32, name="xg", align_bytes=64)
+        for t in range(PACK):
+            nc.vector.tensor_copy(xg[:, t * J : (t + 1) * J], x_planes[t][:].indirect(list1[:]))
+
+        picked = keep.tile([P, PACK * I], F32, name="picked", tag="x%d" % (PACK - 1), align_bytes=64)
+        picked_bf = keep.tile([P, PACK * I], BF16, name="picked_bf", align_bytes=64)
+        picked_codes = keep.tile([P, I], U32, name="picked_codes", align_bytes=64)
+        picked_sc = keep.tile([P, I], U8, name="picked_sc", align_bytes=64)
+        q_sb = [keep.tile([P, I], F32, name="q_sb%d" % m) for m in range(TILES)]
+        xg_bf = keep.tile([P, PACK * J], BF16, name="xg_bf", align_bytes=64)
+        xg_codes = keep.tile([P, J], U32, name="xg_codes", align_bytes=64)
+        xg_sc = keep.tile([P, J], U8, name="xg_sc", align_bytes=64)
+
+        def list2_part(lo, hi):
+            return list2[:, lo // 16 : hi // 16]
+
+        def pick(h):
+            for t in range(PACK):
+                at = (h * PACK + t) * HALF
+                nc.vector.tensor_copy(picked[:, at : at + HALF],
+                                      xg[:, t * J : (t + 1) * J].indirect(list2_part(h * HALF, (h + 1) * HALF)))
+
+        def quantise_picked(h):
+            span = slice(h * PACK * HALF, (h + 1) * PACK * HALF)
+            cols = slice(h * HALF, (h + 1) * HALF)
+            interleave(nc, picked_bf[:, span], picked[:, span].rearrange("p (t c) -> p t c", t=PACK), HALF)
+            nc.vector.quantize_mx(out=picked_codes[:, cols].bitcast(FP8X4), scales=picked_sc[:, cols], in_=picked_bf[:, span])
+
+        def expert(m, lo, hi):
+            acc = q_psum.tile([P, BANK], F32, name="q_acc")
+            nc.tensor.matmul_mx(out=acc[:, 0 : hi - lo], lhsT=wb_codes[:, m * P : (m + 1) * P].bitcast(FP8X4),
+                                lhsT_scale=wb_sc[:, m * P : (m + 1) * P], rhs=picked_codes[:, lo:hi].bitcast(FP8X4),
+                                rhs_scale=picked_sc[:, lo:hi], start=True, stop=True)
+            nc.scalar.copy(out=q_sb[m][:, lo:hi], in_=acc[:, 0 : hi - lo])
+
+        def scatter(m, lo, hi):
+            nc.vector.tensor_copy(pages[m][:].indirect(list2_part(lo, hi)), q_sb[m][:, lo:hi])
+
+        def quantise_group(c):
+            cols = slice(c * BANK, (c + 1) * BANK)
+            span = slice(c * PACK * BANK, (c + 1) * PACK * BANK)
+            interleave(nc, xg_bf[:, span], xg[:].rearrange("p (t c) -> p t c", t=PACK)[:, :, cols], BANK)
+            nc.vector.quantize_mx(out=xg_codes[:, cols].bitcast(FP8X4), scales=xg_sc[:, cols], in_=xg_bf[:, span])
+
+        def finish(m):
+            for c in range(J // BANK):
+                cols = slice(c * BANK, (c + 1) * BANK)
+                acc = p_psum.tile([P, BANK], F32, name="p_acc")
+                nc.tensor.matmul_mx(out=acc[:], lhsT=wa_codes[:, 2 * m * P : 2 * (m + 1) * P].bitcast(FP4X4),
+                                    lhsT_scale=wa_sc[:, m * P : (m + 1) * P], rhs=xg_codes[:, cols].bitcast(FP8X4),
+                                    rhs_scale=xg_sc[:, cols], start=True, stop=True)
+                total = stage.tile([P, BANK], F32, name="total")
+                nc.vector.tensor_tensor(total[:], acc[:], pages[m][:, cols], ADD)
+                nc.sync.dma_start(out=out[m * P : (m + 1) * P, cols], in_=total[:])
+
+        pick(0)
+        quantise_picked(0)
+        expert(0, 0, HALF)
+        expert(1, 0, HALF)
+        pick(1)
+        scatter(0, 0, HALF)
+        quantise_picked(1)
+        expert(0, HALF, I)
+        expert(1, HALF, I)
+        scatter(1, 0, HALF)
+        expert(2, 0, I)
+        expert(3, 0, I)
+        quantise_group(0)
+        quantise_group(1)
+        scatter(0, HALF, I)
+        finish(0)
+        scatter(1, HALF, I)
+        finish(1)
+        for m in range(2, TILES):
+            scatter(m, 0, I)
+            finish(m)

@@ -21,6 +21,7 @@ BANK = 512
 HALF = I // 2
 TILES = N // P
 LINE = 4
+SHARE = 192
 
 
 def interleave(nc, dst, planes, width):
@@ -65,14 +66,15 @@ def tile_list_two_level_routing_kernel(tc, xf, wa_words, wa_scales, wb_words, wb
 
         pages = [keep.tile([P, J], F32, name="page%d" % m) for m in range(TILES)]
         for m in range(TILES):
-            nc.gpsimd.memset(pages[m][:], 0.0)
+            (nc.vector if m == 0 else nc.gpsimd).memset(pages[m][:], 0.0)
 
         xg = keep.tile([P, PACK * J], F32, name="xg", align_bytes=64)
         for t in range(PACK):
             nc.vector.tensor_copy(xg[:, t * J : (t + 1) * J], x_planes[t][:].indirect(list1[:]))
 
         picked = keep.tile([P, PACK * I], F32, name="picked", tag="x%d" % (PACK - 1), align_bytes=64)
-        picked_bf = keep.tile([P, PACK * I], BF16, name="picked_bf", align_bytes=64)
+        late_bf = keep.tile([P, PACK * HALF], BF16, name="late_bf", align_bytes=64)
+        picked_bf = [picked[:, (2 * PACK - 2) * HALF :].bitcast(BF16), late_bf[:]]
         picked_codes = keep.tile([P, I], U32, name="picked_codes", align_bytes=64)
         picked_sc = keep.tile([P, I], U8, name="picked_sc", align_bytes=64)
         q_sb = [keep.tile([P, I], F32, name="q_sb%d" % m) for m in range(TILES)]
@@ -92,8 +94,8 @@ def tile_list_two_level_routing_kernel(tc, xf, wa_words, wa_scales, wb_words, wb
         def quantise_picked(h):
             span = slice(h * PACK * HALF, (h + 1) * PACK * HALF)
             cols = slice(h * HALF, (h + 1) * HALF)
-            interleave(nc, picked_bf[:, span], picked[:, span].rearrange("p (t c) -> p t c", t=PACK), HALF)
-            nc.vector.quantize_mx(out=picked_codes[:, cols].bitcast(FP8X4), scales=picked_sc[:, cols], in_=picked_bf[:, span])
+            interleave(nc, picked_bf[h], picked[:, span].rearrange("p (t c) -> p t c", t=PACK), HALF)
+            nc.vector.quantize_mx(out=picked_codes[:, cols].bitcast(FP8X4), scales=picked_sc[:, cols], in_=picked_bf[h])
 
         def expert(m, lo, hi):
             acc = q_psum.tile([P, BANK], F32, name="q_acc")
@@ -105,41 +107,70 @@ def tile_list_two_level_routing_kernel(tc, xf, wa_words, wa_scales, wb_words, wb
         def scatter(m, lo, hi):
             nc.vector.tensor_copy(pages[m][:].indirect(list2_part(lo, hi)), q_sb[m][:, lo:hi])
 
+        def weave_group(c):
+            cols = slice(c * HALF, (c + 1) * HALF)
+            span = slice(c * PACK * HALF, (c + 1) * PACK * HALF)
+            interleave(nc, xg_bf[:, span], xg[:].rearrange("p (t c) -> p t c", t=PACK)[:, :, cols], HALF)
+
         def quantise_group(c):
             cols = slice(c * BANK, (c + 1) * BANK)
             span = slice(c * PACK * BANK, (c + 1) * PACK * BANK)
-            interleave(nc, xg_bf[:, span], xg[:].rearrange("p (t c) -> p t c", t=PACK)[:, :, cols], BANK)
             nc.vector.quantize_mx(out=xg_codes[:, cols].bitcast(FP8X4), scales=xg_sc[:, cols], in_=xg_bf[:, span])
+
+        def group(m, c):
+            cols = slice(c * BANK, (c + 1) * BANK)
+            acc = p_psum.tile([P, BANK], F32, name="p_acc")
+            nc.tensor.matmul_mx(out=acc[:], lhsT=wa_codes[:, 2 * m * P : 2 * (m + 1) * P].bitcast(FP4X4),
+                                lhsT_scale=wa_sc[:, m * P : (m + 1) * P], rhs=xg_codes[:, cols].bitcast(FP8X4),
+                                rhs_scale=xg_sc[:, cols], start=True, stop=True)
+            return acc
+
+        def add_on_gpsimd(m, c, acc, lo, hi):
+            at = slice(c * BANK + lo, c * BANK + hi)
+            p_sb = stage.tile([P, BANK], F32, name="p_sb", bufs=7)
+            total = stage.tile([P, BANK], F32, name="total")
+            nc.scalar.copy(out=p_sb[:, lo:hi], in_=acc[:, lo:hi])
+            nc.gpsimd.tensor_tensor(total[:, lo:hi], p_sb[:, lo:hi], pages[m][:, at], ADD)
+            nc.sync.dma_start(out=out[m * P : (m + 1) * P, at], in_=total[:, lo:hi])
+
+        def add_on_vector(m, c, acc, lo, hi):
+            at = slice(c * BANK + lo, c * BANK + hi)
+            last = stage.tile([P, HALF], F32, name="last")
+            nc.vector.tensor_tensor(last[:, 0 : hi - lo], acc[:, lo:hi], pages[m][:, at], ADD)
+            nc.scalar.dma_start(out=out[m * P : (m + 1) * P, at], in_=last[:, 0 : hi - lo])
 
         def finish(m):
             for c in range(J // BANK):
-                cols = slice(c * BANK, (c + 1) * BANK)
-                acc = p_psum.tile([P, BANK], F32, name="p_acc")
-                nc.tensor.matmul_mx(out=acc[:], lhsT=wa_codes[:, 2 * m * P : 2 * (m + 1) * P].bitcast(FP4X4),
-                                    lhsT_scale=wa_sc[:, m * P : (m + 1) * P], rhs=xg_codes[:, cols].bitcast(FP8X4),
-                                    rhs_scale=xg_sc[:, cols], start=True, stop=True)
-                total = stage.tile([P, BANK], F32, name="total")
-                nc.vector.tensor_tensor(total[:], acc[:], pages[m][:, cols], ADD)
-                nc.sync.dma_start(out=out[m * P : (m + 1) * P, cols], in_=total[:])
+                add_on_gpsimd(m, c, group(m, c), 0, BANK)
 
         pick(0)
         quantise_picked(0)
         expert(0, 0, HALF)
-        expert(1, 0, HALF)
         pick(1)
         scatter(0, 0, HALF)
         quantise_picked(1)
-        expert(0, HALF, I)
-        expert(1, HALF, I)
+        expert(1, 0, HALF)
         scatter(1, 0, HALF)
+        expert(0, HALF, I)
+        weave_group(0)
+        weave_group(1)
+        quantise_group(0)
+        weave_group(2)
+        weave_group(3)
+        quantise_group(1)
+        expert(1, HALF, I)
+        scatter(0, HALF, I)
         expert(2, 0, I)
         expert(3, 0, I)
-        quantise_group(0)
-        quantise_group(1)
-        scatter(0, HALF, I)
         finish(0)
         scatter(1, HALF, I)
         finish(1)
-        for m in range(2, TILES):
-            scatter(m, 0, I)
-            finish(m)
+        scatter(2, 0, I)
+        finish(2)
+        m = TILES - 1
+        scatter(m, 0, I)
+        left, right = group(m, 0), group(m, 1)
+        add_on_gpsimd(m, 1, right, SHARE, BANK)
+        add_on_vector(m, 0, left, 0, HALF)
+        add_on_vector(m, 0, left, HALF, BANK)
+        add_on_vector(m, 1, right, 0, SHARE)

@@ -107,10 +107,8 @@ def tile_list_two_level_routing_kernel(tc, xf, wa_words, wa_scales, wb_words, wb
         def scatter(m, lo, hi):
             nc.vector.tensor_copy(pages[m][:].indirect(list2_part(lo, hi)), q_sb[m][:, lo:hi])
 
-        def weave_group(c):
-            cols = slice(c * HALF, (c + 1) * HALF)
-            span = slice(c * PACK * HALF, (c + 1) * PACK * HALF)
-            interleave(nc, xg_bf[:, span], xg[:].rearrange("p (t c) -> p t c", t=PACK)[:, :, cols], HALF)
+        def weave_group(lo, hi):
+            interleave(nc, xg_bf[:, PACK * lo : PACK * hi], xg[:].rearrange("p (t c) -> p t c", t=PACK)[:, :, lo:hi], hi - lo)
 
         def quantise_group(c):
             cols = slice(c * BANK, (c + 1) * BANK)
@@ -151,20 +149,19 @@ def tile_list_two_level_routing_kernel(tc, xf, wa_words, wa_scales, wb_words, wb
         quantise_picked(1)
         expert(1, 0, HALF)
         scatter(1, 0, HALF)
-        expert(0, HALF, I)
-        weave_group(0)
-        weave_group(1)
+        weave_group(0, BANK)
         quantise_group(0)
-        weave_group(2)
-        weave_group(3)
+        weave_group(BANK, BANK + HALF)
+        expert(0, HALF, I)
+        weave_group(BANK + HALF, J)
         quantise_group(1)
         expert(1, HALF, I)
         scatter(0, HALF, I)
-        expert(2, 0, I)
-        expert(3, 0, I)
         finish(0)
+        expert(2, 0, I)
         scatter(1, HALF, I)
         finish(1)
+        expert(3, 0, I)
         scatter(2, 0, I)
         finish(2)
         m = TILES - 1

@@ -17,18 +17,33 @@ ADD = mybir.AluOpType.add
 
 P = 128
 PACK = 4
+PER_COLUMN = 16
+QUADRANTS = 4
 BANK = 512
 HALF = I // 2
+QUARTER = J // 4
 TILES = N // P
 LINE = 4
-SHARE = 192
+PICKED_SCALE_ROW = 4
 
 
-def interleave(nc, dst, planes, width):
+def interleave(nc, dst, planes):
     nc.scalar.copy(
         out=dst.rearrange("p (c i t) -> p c t i", i=LINE, t=PACK),
         in_=planes.rearrange("p t (c i) -> p c t i", i=LINE),
     )
+
+
+def load_scales(nc, tile, scales):
+    for quad in range(QUADRANTS):
+        nc.sync.dma_start(
+            out=tile[32 * quad : 32 * quad + 4, :].bitcast(I32),
+            in_=scales[0, 4 * quad : 4 * quad + 4, :].bitcast(I32),
+        )
+
+
+def entries(list_tile, lo, hi):
+    return list_tile[:, lo // PER_COLUMN : hi // PER_COLUMN]
 
 
 def tile_list_two_level_routing_kernel(tc, xf, wa_words, wa_scales, wb_words, wb_scales, offs, offs2, out):
@@ -39,8 +54,8 @@ def tile_list_two_level_routing_kernel(tc, xf, wa_words, wa_scales, wb_words, wb
         q_psum = ctx.enter_context(tc.psum_pool(name="q_psum", bufs=4))
         p_psum = ctx.enter_context(tc.psum_pool(name="p_psum", bufs=4))
 
-        list1 = keep.tile([P, J // 16], U16, name="list1")
-        list2 = keep.tile([P, I // 16], U16, name="list2")
+        list1 = keep.tile([P, J // PER_COLUMN], U16, name="list1")
+        list2 = keep.tile([P, I // PER_COLUMN], U16, name="list2")
         wa_codes = keep.tile([P, 2 * N], U8, name="wa_codes", align_bytes=64)
         wb_codes = keep.tile([P, N], U32, name="wb_codes", align_bytes=64)
         wa_sc = keep.tile([P, N], U8, name="wa_sc", align_bytes=64)
@@ -56,86 +71,99 @@ def tile_list_two_level_routing_kernel(tc, xf, wa_words, wa_scales, wb_words, wb
             nc.sync.dma_start(out=x_planes[t][:], in_=x_rows[:, t, :])
         nc.sync.dma_start(list2[:], offs2)
         nc.sync.dma_start(out=wb_codes[:].bitcast(I32), in_=wb_words[0].rearrange("p n t -> p (n t)").bitcast(I32))
-        for quad in range(4):
-            nc.sync.dma_start(out=wb_sc[32 * quad : 32 * quad + 4, :].bitcast(I32),
-                              in_=wb_scales[0, 4 * quad : 4 * quad + 4, :].bitcast(I32))
+        load_scales(nc, wb_sc, wb_scales)
         nc.sync.dma_start(out=wa_codes[:].bitcast(I32), in_=wa_words[0].bitcast(I32))
-        for quad in range(4):
-            nc.sync.dma_start(out=wa_sc[32 * quad : 32 * quad + 4, :].bitcast(I32),
-                              in_=wa_scales[0, 4 * quad : 4 * quad + 4, :].bitcast(I32))
+        load_scales(nc, wa_sc, wa_scales)
 
         pages = [keep.tile([P, J], F32, name="page%d" % m) for m in range(TILES)]
-        for m in range(TILES):
-            (nc.vector if m == 0 else nc.gpsimd).memset(pages[m][:], 0.0)
+        nc.vector.memset(pages[0][:], 0.0)
+        for m in range(1, TILES):
+            nc.gpsimd.memset(pages[m][:], 0.0)
 
         xg = keep.tile([P, PACK * J], F32, name="xg", align_bytes=64)
         for t in range(PACK):
-            nc.vector.tensor_copy(xg[:, t * J : (t + 1) * J], x_planes[t][:].indirect(list1[:]))
+            step = J if t < PACK - 1 else BANK
+            for lo in range(0, J, step):
+                nc.vector.tensor_copy(
+                    xg[:, t * J + lo : t * J + lo + step], x_planes[t][:].indirect(entries(list1, lo, lo + step))
+                )
 
-        picked = keep.tile([P, PACK * I], F32, name="picked", tag="x%d" % (PACK - 1), align_bytes=64)
+        picked = keep.tile([P, PACK * I + HALF], F32, name="picked", tag="x%d" % (PACK - 1), align_bytes=64)
         late_bf = keep.tile([P, PACK * HALF], BF16, name="late_bf", align_bytes=64)
-        picked_bf = [picked[:, (2 * PACK - 2) * HALF :].bitcast(BF16), late_bf[:]]
+        picked_bf = [picked[:, PACK * I - HALF :].bitcast(BF16), late_bf[:]]
         picked_codes = keep.tile([P, I], U32, name="picked_codes", align_bytes=64)
-        picked_sc = keep.tile([P, I], U8, name="picked_sc", align_bytes=64)
         q_sb = [keep.tile([P, I], F32, name="q_sb%d" % m) for m in range(TILES)]
         xg_bf = keep.tile([P, PACK * J], BF16, name="xg_bf", align_bytes=64)
         xg_codes = keep.tile([P, J], U32, name="xg_codes", align_bytes=64)
         xg_sc = keep.tile([P, J], U8, name="xg_sc", align_bytes=64)
-
-        def list2_part(lo, hi):
-            return list2[:, lo // 16 : hi // 16]
+        picked_sc = xg_sc[PICKED_SCALE_ROW:P, 0:I]
 
         def pick(h):
             for t in range(PACK):
                 at = (h * PACK + t) * HALF
-                nc.vector.tensor_copy(picked[:, at : at + HALF],
-                                      xg[:, t * J : (t + 1) * J].indirect(list2_part(h * HALF, (h + 1) * HALF)))
+                window = xg[:, t * J : (t + 1) * J]
+                nc.vector.tensor_copy(picked[:, at : at + HALF], window.indirect(entries(list2, h * HALF, (h + 1) * HALF)))
 
         def quantise_picked(h):
-            span = slice(h * PACK * HALF, (h + 1) * PACK * HALF)
+            planes = picked[:, h * PACK * HALF : (h + 1) * PACK * HALF].rearrange("p (t c) -> p t c", t=PACK)
             cols = slice(h * HALF, (h + 1) * HALF)
-            interleave(nc, picked_bf[h], picked[:, span].rearrange("p (t c) -> p t c", t=PACK), HALF)
+            interleave(nc, picked_bf[h], planes)
             nc.vector.quantize_mx(out=picked_codes[:, cols].bitcast(FP8X4), scales=picked_sc[:, cols], in_=picked_bf[h])
 
         def expert(m, lo, hi):
             acc = q_psum.tile([P, BANK], F32, name="q_acc")
-            nc.tensor.matmul_mx(out=acc[:, 0 : hi - lo], lhsT=wb_codes[:, m * P : (m + 1) * P].bitcast(FP8X4),
-                                lhsT_scale=wb_sc[:, m * P : (m + 1) * P], rhs=picked_codes[:, lo:hi].bitcast(FP8X4),
-                                rhs_scale=picked_sc[:, lo:hi], start=True, stop=True)
+            nc.tensor.matmul_mx(
+                out=acc[:, 0 : hi - lo],
+                lhsT=wb_codes[:, m * P : (m + 1) * P].bitcast(FP8X4),
+                lhsT_scale=wb_sc[:, m * P : (m + 1) * P],
+                rhs=picked_codes[:, lo:hi].bitcast(FP8X4),
+                rhs_scale=picked_sc[:, lo:hi],
+                start=True,
+                stop=True,
+            )
             nc.scalar.copy(out=q_sb[m][:, lo:hi], in_=acc[:, 0 : hi - lo])
 
         def scatter(m, lo, hi):
-            nc.vector.tensor_copy(pages[m][:].indirect(list2_part(lo, hi)), q_sb[m][:, lo:hi])
+            nc.vector.tensor_copy(pages[m][:].indirect(entries(list2, lo, hi)), q_sb[m][:, lo:hi])
 
-        def weave_group(lo, hi):
-            interleave(nc, xg_bf[:, PACK * lo : PACK * hi], xg[:].rearrange("p (t c) -> p t c", t=PACK)[:, :, lo:hi], hi - lo)
+        def interleave_group(lo, hi):
+            interleave(nc, xg_bf[:, PACK * lo : PACK * hi], xg[:].rearrange("p (t c) -> p t c", t=PACK)[:, :, lo:hi])
 
         def quantise_group(c):
             cols = slice(c * BANK, (c + 1) * BANK)
-            span = slice(c * PACK * BANK, (c + 1) * PACK * BANK)
-            nc.vector.quantize_mx(out=xg_codes[:, cols].bitcast(FP8X4), scales=xg_sc[:, cols], in_=xg_bf[:, span])
+            nc.vector.quantize_mx(
+                out=xg_codes[:, cols].bitcast(FP8X4),
+                scales=xg_sc[:, cols],
+                in_=xg_bf[:, c * PACK * BANK : (c + 1) * PACK * BANK],
+            )
 
         def group(m, c):
             cols = slice(c * BANK, (c + 1) * BANK)
             acc = p_psum.tile([P, BANK], F32, name="p_acc")
-            nc.tensor.matmul_mx(out=acc[:], lhsT=wa_codes[:, 2 * m * P : 2 * (m + 1) * P].bitcast(FP4X4),
-                                lhsT_scale=wa_sc[:, m * P : (m + 1) * P], rhs=xg_codes[:, cols].bitcast(FP8X4),
-                                rhs_scale=xg_sc[:, cols], start=True, stop=True)
+            nc.tensor.matmul_mx(
+                out=acc[:],
+                lhsT=wa_codes[:, 2 * m * P : 2 * (m + 1) * P].bitcast(FP4X4),
+                lhsT_scale=wa_sc[:, m * P : (m + 1) * P],
+                rhs=xg_codes[:, cols].bitcast(FP8X4),
+                rhs_scale=xg_sc[:, cols],
+                start=True,
+                stop=True,
+            )
             return acc
 
         def add_on_gpsimd(m, c, acc, lo, hi):
             at = slice(c * BANK + lo, c * BANK + hi)
-            p_sb = stage.tile([P, BANK], F32, name="p_sb", bufs=7)
+            p_sb = stage.tile([P, BANK], F32, name="p_sb", bufs=2 * TILES - 1)
             total = stage.tile([P, BANK], F32, name="total")
             nc.scalar.copy(out=p_sb[:, lo:hi], in_=acc[:, lo:hi])
             nc.gpsimd.tensor_tensor(total[:, lo:hi], p_sb[:, lo:hi], pages[m][:, at], ADD)
             nc.sync.dma_start(out=out[m * P : (m + 1) * P, at], in_=total[:, lo:hi])
 
-        def add_on_vector(m, c, acc, lo, hi):
-            at = slice(c * BANK + lo, c * BANK + hi)
-            last = stage.tile([P, HALF], F32, name="last")
-            nc.vector.tensor_tensor(last[:, 0 : hi - lo], acc[:, lo:hi], pages[m][:, at], ADD)
-            nc.scalar.dma_start(out=out[m * P : (m + 1) * P, at], in_=last[:, 0 : hi - lo])
+        def add_on_vector(m, c, acc, lo):
+            at = slice(c * BANK + lo, c * BANK + lo + QUARTER)
+            last = stage.tile([P, QUARTER], F32, name="last")
+            nc.vector.tensor_tensor(last[:], acc[:, lo : lo + QUARTER], pages[m][:, at], ADD)
+            nc.scalar.dma_start(out=out[m * P : (m + 1) * P, at], in_=last[:])
 
         def finish(m):
             for c in range(J // BANK):
@@ -145,17 +173,18 @@ def tile_list_two_level_routing_kernel(tc, xf, wa_words, wa_scales, wb_words, wb
         quantise_picked(0)
         expert(0, 0, HALF)
         pick(1)
+        interleave_group(0, BANK)
+        quantise_group(0)
         scatter(0, 0, HALF)
         quantise_picked(1)
         expert(1, 0, HALF)
         scatter(1, 0, HALF)
-        weave_group(0, BANK)
-        quantise_group(0)
-        weave_group(BANK, BANK + HALF)
+        interleave_group(BANK, BANK + QUARTER)
         expert(0, HALF, I)
-        weave_group(BANK + HALF, J)
+        interleave_group(BANK + QUARTER, J)
         quantise_group(1)
         expert(1, HALF, I)
+
         scatter(0, HALF, I)
         finish(0)
         expert(2, 0, I)
@@ -164,10 +193,11 @@ def tile_list_two_level_routing_kernel(tc, xf, wa_words, wa_scales, wb_words, wb
         expert(3, 0, I)
         scatter(2, 0, I)
         finish(2)
+
         m = TILES - 1
         scatter(m, 0, I)
         left, right = group(m, 0), group(m, 1)
-        add_on_gpsimd(m, 1, right, SHARE, BANK)
-        add_on_vector(m, 0, left, 0, HALF)
-        add_on_vector(m, 0, left, HALF, BANK)
-        add_on_vector(m, 1, right, 0, SHARE)
+        add_on_gpsimd(m, 1, right, QUARTER, BANK)
+        add_on_vector(m, 0, left, 0)
+        add_on_vector(m, 0, left, QUARTER)
+        add_on_vector(m, 1, right, 0)

from contextlib import ExitStack

import concourse.mybir as mybir

K, T, J, I, N = 512, 2048, 1024, 512, 512
FLOPS = 2 * K * N * (J + I)

F32 = mybir.dt.float32
BF16 = mybir.dt.bfloat16
I32 = mybir.dt.int32
U32 = mybir.dt.uint32
U16 = mybir.dt.uint16
U8 = mybir.dt.uint8
FP8X4 = mybir.dt.float8_e4m3fn_x4
FP4X4 = mybir.dt.float4_e2m1fn_x4
ADD = mybir.AluOpType.add

P = 128
PACK = 4
PER_COLUMN = 16
QUADRANTS = 4
BANK = 512
HALF = I // 2
QUARTER = J // 4
TILES = N // P
LINE = 4
PICKED_SCALE_ROW = 4


def interleave(nc, dst, planes):
    nc.scalar.copy(
        out=dst.rearrange("p (c i t) -> p c t i", i=LINE, t=PACK),
        in_=planes.rearrange("p t (c i) -> p c t i", i=LINE),
    )


def load_scales(nc, tile, scales):
    for quad in range(QUADRANTS):
        nc.sync.dma_start(
            out=tile[32 * quad : 32 * quad + 4, :].bitcast(I32),
            in_=scales[0, 4 * quad : 4 * quad + 4, :].bitcast(I32),
        )


def entries(list_tile, lo, hi):
    return list_tile[:, lo // PER_COLUMN : hi // PER_COLUMN]


def tile_list_two_level_routing_kernel(tc, xf, wa_words, wa_scales, wb_words, wb_scales, offs, offs2, out):
    nc = tc.nc
    with ExitStack() as ctx:
        keep = ctx.enter_context(tc.tile_pool(name="keep", bufs=1))
        stage = ctx.enter_context(tc.tile_pool(name="stage", bufs=4))
        q_psum = ctx.enter_context(tc.psum_pool(name="q_psum", bufs=4))
        p_psum = ctx.enter_context(tc.psum_pool(name="p_psum", bufs=4))

        list1 = keep.tile([P, J // PER_COLUMN], U16, name="list1")
        list2 = keep.tile([P, I // PER_COLUMN], U16, name="list2")
        wa_codes = keep.tile([P, 2 * N], U8, name="wa_codes", align_bytes=64)
        wb_codes = keep.tile([P, N], U32, name="wb_codes", align_bytes=64)
        wa_sc = keep.tile([P, N], U8, name="wa_sc", align_bytes=64)
        wb_sc = keep.tile([P, N], U8, name="wb_sc", align_bytes=64)
        nc.vector.memset(wb_sc[:].bitcast(U32), 0)
        nc.vector.memset(wa_sc[:].bitcast(U32), 0)

        x_rows = xf.rearrange("(p t) c -> p t c", t=PACK)
        x_planes = [keep.tile([P, T], F32, name="x%d" % t, tag="x%d" % t, align_bytes=64) for t in range(PACK)]
        nc.sync.dma_start(out=x_planes[0][:], in_=x_rows[:, 0, :])
        nc.sync.dma_start(list1[:], offs)
        for t in range(1, PACK):
            nc.sync.dma_start(out=x_planes[t][:], in_=x_rows[:, t, :])
        nc.sync.dma_start(list2[:], offs2)
        nc.sync.dma_start(out=wb_codes[:].bitcast(I32), in_=wb_words[0].rearrange("p n t -> p (n t)").bitcast(I32))
        load_scales(nc, wb_sc, wb_scales)
        nc.sync.dma_start(out=wa_codes[:].bitcast(I32), in_=wa_words[0].bitcast(I32))
        load_scales(nc, wa_sc, wa_scales)

        pages = [keep.tile([P, J], F32, name="page%d" % m) for m in range(TILES)]
        nc.vector.memset(pages[0][:], 0.0)
        for m in range(1, TILES):
            nc.gpsimd.memset(pages[m][:], 0.0)

        xg = keep.tile([P, PACK * J], F32, name="xg", align_bytes=64)
        for t in range(PACK):
            step = J if t < PACK - 1 else BANK
            for lo in range(0, J, step):
                nc.vector.tensor_copy(
                    xg[:, t * J + lo : t * J + lo + step], x_planes[t][:].indirect(entries(list1, lo, lo + step))
                )

        picked = keep.tile([P, PACK * I + HALF], F32, name="picked", tag="x%d" % (PACK - 1), align_bytes=64)
        late_bf = keep.tile([P, PACK * HALF], BF16, name="late_bf", align_bytes=64)
        picked_bf = [picked[:, PACK * I - HALF :].bitcast(BF16), late_bf[:]]
        picked_codes = keep.tile([P, I], U32, name="picked_codes", align_bytes=64)
        q_sb = [keep.tile([P, I], F32, name="q_sb%d" % m) for m in range(TILES)]
        xg_bf = keep.tile([P, PACK * J], BF16, name="xg_bf", align_bytes=64)
        xg_codes = keep.tile([P, J], U32, name="xg_codes", align_bytes=64)
        xg_sc = keep.tile([P, J], U8, name="xg_sc", align_bytes=64)
        picked_sc = xg_sc[PICKED_SCALE_ROW:P, 0:I]

        def pick(h):
            for t in range(PACK):
                at = (h * PACK + t) * HALF
                window = xg[:, t * J : (t + 1) * J]
                nc.vector.tensor_copy(picked[:, at : at + HALF], window.indirect(entries(list2, h * HALF, (h + 1) * HALF)))

        def quantise_picked(h):
            planes = picked[:, h * PACK * HALF : (h + 1) * PACK * HALF].rearrange("p (t c) -> p t c", t=PACK)
            cols = slice(h * HALF, (h + 1) * HALF)
            interleave(nc, picked_bf[h], planes)
            nc.vector.quantize_mx(out=picked_codes[:, cols].bitcast(FP8X4), scales=picked_sc[:, cols], in_=picked_bf[h])

        def expert(m, lo, hi):
            acc = q_psum.tile([P, BANK], F32, name="q_acc")
            nc.tensor.matmul_mx(
                out=acc[:, 0 : hi - lo],
                lhsT=wb_codes[:, m * P : (m + 1) * P].bitcast(FP8X4),
                lhsT_scale=wb_sc[:, m * P : (m + 1) * P],
                rhs=picked_codes[:, lo:hi].bitcast(FP8X4),
                rhs_scale=picked_sc[:, lo:hi],
                start=True,
                stop=True,
            )
            nc.scalar.copy(out=q_sb[m][:, lo:hi], in_=acc[:, 0 : hi - lo])

        def scatter(m, lo, hi):
            nc.vector.tensor_copy(pages[m][:].indirect(entries(list2, lo, hi)), q_sb[m][:, lo:hi])

        def interleave_group(lo, hi):
            interleave(nc, xg_bf[:, PACK * lo : PACK * hi], xg[:].rearrange("p (t c) -> p t c", t=PACK)[:, :, lo:hi])

        def quantise_group(c):
            cols = slice(c * BANK, (c + 1) * BANK)
            nc.vector.quantize_mx(
                out=xg_codes[:, cols].bitcast(FP8X4),
                scales=xg_sc[:, cols],
                in_=xg_bf[:, c * PACK * BANK : (c + 1) * PACK * BANK],
            )

        def group(m, c):
            cols = slice(c * BANK, (c + 1) * BANK)
            acc = p_psum.tile([P, BANK], F32, name="p_acc")
            nc.tensor.matmul_mx(
                out=acc[:],
                lhsT=wa_codes[:, 2 * m * P : 2 * (m + 1) * P].bitcast(FP4X4),
                lhsT_scale=wa_sc[:, m * P : (m + 1) * P],
                rhs=xg_codes[:, cols].bitcast(FP8X4),
                rhs_scale=xg_sc[:, cols],
                start=True,
                stop=True,
            )
            return acc

        def add_on_gpsimd(m, c, acc, lo, hi):
            at = slice(c * BANK + lo, c * BANK + hi)
            p_sb = stage.tile([P, BANK], F32, name="p_sb", bufs=2 * TILES - 1)
            total = stage.tile([P, BANK], F32, name="total")
            nc.scalar.copy(out=p_sb[:, lo:hi], in_=acc[:, lo:hi])
            nc.gpsimd.tensor_tensor(total[:, lo:hi], p_sb[:, lo:hi], pages[m][:, at], ADD)
            nc.sync.dma_start(out=out[m * P : (m + 1) * P, at], in_=total[:, lo:hi])

        def add_on_vector(m, c, acc, lo):
            at = slice(c * BANK + lo, c * BANK + lo + QUARTER)
            last = stage.tile([P, QUARTER], F32, name="last")
            nc.vector.tensor_tensor(last[:], acc[:, lo : lo + QUARTER], pages[m][:, at], ADD)
            nc.scalar.dma_start(out=out[m * P : (m + 1) * P, at], in_=last[:])

        def finish(m):
            for c in range(J // BANK):
                add_on_gpsimd(m, c, group(m, c), 0, BANK)

        pick(0)
        quantise_picked(0)
        expert(0, 0, HALF)
        pick(1)
        interleave_group(0, BANK)
        quantise_group(0)
        scatter(0, 0, HALF)
        quantise_picked(1)
        expert(1, 0, HALF)
        scatter(1, 0, HALF)
        interleave_group(BANK, BANK + QUARTER)
        expert(0, HALF, I)
        interleave_group(BANK + QUARTER, J)
        quantise_group(1)
        expert(1, HALF, I)

        scatter(0, HALF, I)
        finish(0)
        expert(2, 0, I)
        scatter(1, HALF, I)
        finish(1)
        expert(3, 0, I)
        scatter(2, 0, I)
        finish(2)

        m = TILES - 1
        scatter(m, 0, I)
        left, right = group(m, 0), group(m, 1)
        add_on_gpsimd(m, 1, right, QUARTER, BANK)
        add_on_vector(m, 0, left, 0)
        add_on_vector(m, 0, left, QUARTER)
        add_on_vector(m, 1, right, 0)
